import numpy as np
import ml_dtypes


def mxq(x, axis, fmt="e4m3"):
    dtype, down = {"e4m3": (ml_dtypes.float8_e4m3fn, 7), "e5m2": (ml_dtypes.float8_e5m2, 14)}[fmt]
    v = np.moveaxis(np.asarray(x, np.float32).astype(ml_dtypes.bfloat16).astype(np.float64), axis, -1)
    blocks = v.reshape(v.shape[:-1] + (-1, 32))
    amax = np.abs(blocks).max(-1, keepdims=True)
    byte = np.maximum(np.where(amax > 0, np.frexp(amax)[1] - 1 + 127, 0) - down, 1)
    scale = np.exp2(byte - 127.0)
    codes = (blocks / scale).astype(np.float32).astype(dtype).astype(np.float64)
    return np.moveaxis((codes * scale).reshape(v.shape), -1, axis)


WIDE = False


def mx_kscale(k):
    if not WIDE:
        return np.ones(k)
    levels = np.array([10, -10, 5, -5, 0])
    if k % 512:
        return np.exp2(np.random.permutation(np.resize(levels, k // 32))).repeat(32)
    a = np.empty((k // 512, 16))
    for p in range(k // 512):
        a[p, :8] = np.random.permutation(np.resize(levels, 8))
        for g in range(8):
            far = levels[np.abs(levels - a[p, g]) >= 10]
            a[p, g + 8] = far[np.random.randint(len(far))]
    return np.exp2(a.ravel()).repeat(32)


BF16 = ml_dtypes.bfloat16


def bf(x):
    return np.asarray(x, np.float32).astype(BF16)


def f64(x):
    return np.asarray(x).astype(np.float64)

E4M3FN = np.array([(-1.0 if i & 128 else 1.0) * ((1.0 + (i & 7) / 8.0) * 2.0 ** (((i >> 3) & 15) - 7) if i & 120 else (i & 7) * 2.0 ** -9) for i in range(256)])


def e4m3fn_bytes(y):
    return np.clip(np.asarray(y, np.float64), -448.0, 448.0).astype(np.float32).astype(ml_dtypes.float8_e4m3fn).view(np.uint8)


def e4m3fn_values(b):
    return E4M3FN[b]


T, K, N, R, G = 1024, 2048, 1536, 512, 128


def setup_inputs():
    s, t = mx_kscale(K), mx_kscale(R)
    x = np.random.standard_normal((T, K)) * np.random.uniform(0.5, 1.5, (T, 1)) * s
    c = np.random.uniform(0.5, 1.5, (K // G, N // G))
    w0 = np.random.standard_normal((K, N)) / np.sqrt(K) * np.repeat(np.repeat(c, G, 0), G, 1) * np.random.uniform(0.5, 1.5, N)
    b0 = 0.5 * np.random.standard_normal((R, N)) / np.sqrt(R)
    lam = 1 + 0.2 * np.random.standard_normal(R)
    norm = np.sqrt((w0 ** 2).sum(0) + ((lam[:, None] * b0) ** 2).sum(0))
    w = w0 / s[:, None]
    x_scale = (np.abs(x).reshape(T, K // G, G).max(2) / 448).astype(np.float32)
    w_scale = (np.abs(w).reshape(K // G, G, N // G, G).max((1, 3)) / 448).astype(np.float32)
    return {"x_bytes": e4m3fn_bytes(x / np.repeat(f64(x_scale), G, 1)),
            "x_scale": x_scale,
            "w_bytes": e4m3fn_bytes(w / np.repeat(np.repeat(f64(w_scale), G, 0), G, 1)),
            "w_scale": w_scale,
            "a": bf(np.random.standard_normal((K, R)) / np.sqrt(K) / s[:, None] * t),
            "lam": bf(lam),
            "b": bf(b0 / t[:, None]),
            "mag": bf(norm * np.random.uniform(0.6, 1.4, N)),
            "norm": bf(norm)}


def reference(x_bytes, x_scale, w_bytes, w_scale, a, lam, b, mag, norm):
    x = e4m3fn_values(x_bytes) * np.repeat(f64(x_scale), G, 1)
    w = e4m3fn_values(w_bytes) * np.repeat(np.repeat(f64(w_scale), G, 0), G, 1)
    xq = mxq(x, 1, "e4m3")
    base = xq @ mxq(w, 0, "e4m3")
    h = (xq @ mxq(f64(a), 0, "e4m3")) * f64(lam)
    delta = mxq(h, 1, "e4m3") @ mxq(f64(b), 0, "e4m3")
    return (base + delta) * (f64(mag) / f64(norm))

from contextlib import ExitStack

import concourse.mybir as mybir
from concourse.masks import make_identity

T, K, N, R = 1024, 2048, 1536, 512
FLOPS = 2 * T * (K * N + K * R + R * N)

F32 = mybir.dt.float32
BF16 = mybir.dt.bfloat16
U32 = mybir.dt.uint32
U8 = mybir.dt.uint8
E4M3 = mybir.dt.float8_e4m3fn
MX = mybir.dt.float8_e4m3fn_x4
MULT = mybir.AluOpType.mult
COPY = mybir.ActivationFunctionType.Copy

P = 128
G = K // 512
TILES = T // P
PAIRS = TILES // 2
CW = 512
C = N // CW


def tile_dora_fp8_forward_d2_kernel(tc, x_bytes, x_scale, w_bytes, w_scale, a, lam, b, mag, norm, out):
    nc = tc.nc
    with ExitStack() as ctx:
        keep = ctx.enter_context(tc.tile_pool(name="keep", bufs=1))
        agp = ctx.enter_context(tc.tile_pool(name="agp", bufs=2))
        xwp = ctx.enter_context(tc.tile_pool(name="xwp", bufs=4))
        xgp = ctx.enter_context(tc.tile_pool(name="xgp", bufs=4))
        wwp = ctx.enter_context(tc.tile_pool(name="wwp", bufs=4))
        wgp = ctx.enter_context(tc.tile_pool(name="wgp", bufs=4))
        hp = ctx.enter_context(tc.tile_pool(name="hp", bufs=2))
        resp = ctx.enter_context(tc.tile_pool(name="resp", bufs=8))
        psum = ctx.enter_context(tc.psum_pool(name="psum", bufs=4))

        def kept(shape, dtype, name):
            return keep.tile(shape, dtype, name=name, align_bytes=64)

        ident = kept([P, P], F32, "ident")
        xs = kept([P, TILES, K // 128], F32, "xs")
        wsall = kept([P, G, 4, N // 128], F32, "wsall")
        ws = kept([P, G, N // 128], F32, "ws")
        lamb = kept([P, 4], BF16, "lamb")
        lamf = kept([P, 4], F32, "lamf")
        magb = kept([P, N // P], BF16, "magb")
        normb = kept([P, N // P], BF16, "normb")
        rec = kept([P, N // P], F32, "rec")
        s1 = kept([P, N // P], F32, "s1")
        sb = kept([P, N], F32, "sb")
        xb = [kept([P, 2, K], U8, f"xb{j}") for j in range(PAIRS)]
        araw = [kept([P, 4, R], BF16, f"araw{g}") for g in range(G)]
        wb = [kept([P, 4, CW], U8, f"wb{v}") for v in range(C * G)]
        braw = [kept([P, 4, CW], BF16, f"braw{c}") for c in range(C)]
        xq = kept([P, G, T], U32, "xq")
        xqs = kept([P, G, T], U8, "xqs")
        aq = kept([P, G, R], U32, "aq")
        aqs = kept([P, G, R], U8, "aqs")
        wq = [kept([P, CW], U32, f"wq{v}") for v in range(C * G)]
        wqs = [kept([P, CW], U8, f"wqs{v}") for v in range(C * G)]
        bq = [kept([P, CW], U32, f"bq{c}") for c in range(C)]
        bqs = [kept([P, CW], U8, f"bqs{c}") for c in range(C)]
        hq = kept([P, T], U32, "hq")
        hqs = kept([P, T], U8, "hqs")

        x_view = x_bytes.rearrange("(p i) k -> p i k", i=TILES)
        a_view = a.rearrange("(g p t) r -> g p t r", p=P, t=4)
        w_view = w_bytes.rearrange("(g p t) n -> g p t n", p=P, t=4)
        b_view = b.rearrange("(p t) n -> p t n", t=4)
        out_view = out.rearrange("(p i) n -> p i n", i=TILES)

        nc.scalar.dma_start(out=xs[:], in_=x_scale.rearrange("(p i) k -> p i k", i=TILES))
        make_identity(nc, ident[:])
        nc.gpsimd.dma_start(out=lamb[:], in_=lam.rearrange("(p t) -> p t", t=4))
        nc.gpsimd.dma_start(out=magb[:], in_=mag.rearrange("(p j) -> p j", j=N // P))
        nc.gpsimd.dma_start(out=normb[:], in_=norm.rearrange("(p j) -> p j", j=N // P))
        nc.gpsimd.dma_start(
            out=wsall[:].rearrange("p g q n -> p (g q n)"),
            in_=w_scale.rearrange("k n -> (k n)").partition_broadcast(P),
        )
        nc.gpsimd.tensor_copy(out=lamf[:], in_=lamb[:])
        for q in range(4):
            rows = slice(32 * q, 32 * q + 32)
            nc.gpsimd.tensor_copy(out=ws[rows, :, :], in_=wsall[rows, :, q, :])

        half = K // 2
        nc.sync.dma_start(out=xb[0][:, :, 0:half], in_=x_view[:, 0:2, 0:half])
        nc.sync.dma_start(out=araw[0][:], in_=a_view[0])
        nc.sync.dma_start(out=xb[0][:, :, half:K], in_=x_view[:, 0:2, half:K])
        nc.sync.dma_start(out=araw[1][:], in_=a_view[1])
        nc.sync.dma_start(out=xb[1][:], in_=x_view[:, 2:4, :])
        nc.sync.dma_start(out=araw[2][:], in_=a_view[2])
        nc.sync.dma_start(out=araw[3][:], in_=a_view[3])
        nc.sync.dma_start(out=xb[2][:], in_=x_view[:, 4:6, :])
        nc.sync.dma_start(out=xb[3][:], in_=x_view[:, 6:8, :])
        for c in range(C):
            cols = slice(CW * c, CW * (c + 1))
            for g in range(G):
                nc.sync.dma_start(out=wb[G * c + g][:], in_=w_view[g][:, :, cols])
                if g == 3:
                    nc.sync.dma_start(out=braw[c][:], in_=b_view[:, :, cols])

        xw, xbank, xg = {}, {}, {}

        def x_widen(u):
            j, g = divmod(u, G)
            xw[u] = xwp.tile([P, 2, 512], BF16, name="xw", align_bytes=64)
            for i in range(2):
                for q in range(4):
                    k = 512 * g + 128 * q
                    nc.vector.tensor_scalar(
                        out=xw[u][:, i, 128 * q : 128 * (q + 1)],
                        in0=xb[j][:, i, k : k + 128].bitcast(E4M3),
                        scalar1=xs[:, 2 * j + i, 4 * g + q : 4 * g + q + 1],
                        scalar2=None,
                        op0=MULT,
                    )

        def x_turn(u):
            xbank[u] = psum.tile([P, 2, 2, P], F32, name="bank", tag="bank")
            for i in range(2):
                words = xw[u][:, i, :].bitcast(F32)
                for h in range(2):
                    nc.tensor.transpose(xbank[u][:, i, h, :], words[:, h:256:2], ident[:])

        def x_out(u):
            xg[u] = xgp.tile([P, 2, P, 4], BF16, name="xg", align_bytes=64)
            nc.scalar.copy(
                out=xg[u][:].rearrange("p i r t -> p (i r t)").bitcast(F32).rearrange("p (i r h) -> p i r h", i=2, h=2),
                in_=xbank[u][:].rearrange("p i h r -> p i r h"),
            )

        def x_quant(u):
            j, g = divmod(u, G)
            cols = slice(256 * j, 256 * (j + 1))
            nc.vector.quantize_mx(
                out=xq[:, g, cols].bitcast(MX),
                scales=xqs[:, g, cols],
                in_=xg[u][:].rearrange("p i r t -> p (i r t)"),
            )

        ag = {}

        def a_inter(g, t, engine):
            if t == 0:
                ag[g] = agp.tile([P, 4, P, 4], BF16, name="ag", align_bytes=64)
            dst = ag[g][:, t, :, :]
            src = araw[g][:].rearrange("p j (m t) -> p t m j", t=4)[:, t, :, :]
            if engine == "v":
                nc.vector.tensor_copy(out=dst, in_=src)
            else:
                nc.scalar.copy(out=dst, in_=src)

        def a_quant(g):
            nc.vector.quantize_mx(
                out=aq[:, g, :].bitcast(MX), scales=aqs[:, g, :], in_=ag[g][:].rearrange("p t m j -> p (t m j)")
            )

        hbank, hb, hg = {}, {}, {}

        def h_mm(j):
            cols = slice(256 * j, 256 * (j + 1))
            for t in range(4):
                if t % 2 == 0:
                    tag = "acc" if j < 2 else "bank"
                    hbank[j, t // 2] = psum.tile([P, 2, 256], F32, name=tag, tag=tag)
                for g in range(G):
                    nc.tensor.matmul_mx(
                        out=hbank[j, t // 2][:, t % 2, :],
                        lhsT=aq[:, g, P * t : P * (t + 1)].bitcast(MX),
                        lhsT_scale=aqs[:, g, P * t : P * (t + 1)],
                        rhs=xq[:, g, cols].bitcast(MX),
                        rhs_scale=xqs[:, g, cols],
                        start=(g == 0),
                        stop=(g == G - 1),
                    )

        def h_out(j):
            hb[j] = hp.tile([P, 4, 256], BF16, name="hb", align_bytes=64)
            for t in range(4):
                nc.scalar.activation(
                    out=hb[j][:, t, :], in_=hbank[j, t // 2][:, t % 2, :], func=COPY, scale=lamf[:, t : t + 1]
                )

        def h_inter(j):
            hg[j] = hp.tile([P, 256, 4], BF16, name="hg", align_bytes=64)
            nc.vector.tensor_copy(out=hg[j][:], in_=hb[j][:].rearrange("p t n -> p n t"))

        def h_quant(j):
            cols = slice(256 * j, 256 * (j + 1))
            nc.vector.quantize_mx(
                out=hq[:, cols].bitcast(MX), scales=hqs[:, cols], in_=hg[j][:].rearrange("p n t -> p (n t)")
            )

        bg = {}

        def b_inter(c, engine):
            bg[c] = wgp.tile([P, CW, 4], BF16, name="wg", tag="wg", align_bytes=64)
            for e in range(2):
                n = slice(256 * e, 256 * (e + 1))
                if engine == "v":
                    nc.vector.tensor_copy(out=bg[c][:, n, :], in_=braw[c][:, :, n].rearrange("p t n -> p n t"))
                else:
                    nc.scalar.copy(out=bg[c][:, n, :], in_=braw[c][:, :, n].rearrange("p t n -> p n t"))

        def b_quant(c):
            nc.vector.quantize_mx(out=bq[c][:].bitcast(MX), scales=bqs[c][:], in_=bg[c][:].rearrange("p n t -> p (n t)"))

        subs = [(0, 512), (512, 512), (1024, 256), (1280, 256)]
        ww, wg, acc = {}, {}, {}

        def w_widen(v, halves=(0, 1)):
            for e in halves:
                if e == 0:
                    ww[v] = wwp.tile([P, 4, CW], BF16, name="ww", align_bytes=64)
                nc.scalar.copy(
                    out=ww[v][:, 2 * e : 2 * e + 2, :].rearrange("p t n -> p (t n)"),
                    in_=wb[v][:, 2 * e : 2 * e + 2, :].rearrange("p t n -> p (t n)").bitcast(E4M3),
                )

        def w_inter(u, g, engine, blocks):
            n0, width = subs[u]
            if (u, g) not in wg:
                wg[u, g] = wgp.tile([P, CW, 4], BF16, name="wg", tag="wg", align_bytes=64)
            for e in blocks:
                src = ww[G * (n0 // CW) + g][:, :, n0 % CW + 128 * e : n0 % CW + 128 * (e + 1)].rearrange("p t n -> p n t")
                dst = wg[u, g][:, 128 * e : 128 * (e + 1), :]
                block = n0 // 128 + e
                scale = ws[:, g, block : block + 1]
                if engine == "v":
                    nc.vector.tensor_scalar(out=dst, in0=src, scalar1=scale, scalar2=None, op0=MULT)
                else:
                    nc.scalar.activation(out=dst, in_=src, func=COPY, scale=scale)

        def w_cols(u, g):
            n0, width = subs[u]
            return G * (n0 // CW) + g, slice(n0 % CW, n0 % CW + width)

        def w_quant(u, g):
            v, cols = w_cols(u, g)
            width = subs[u][1]
            nc.vector.quantize_mx(
                out=wq[v][:, cols].bitcast(MX),
                scales=wqs[v][:, cols],
                in_=wg[u, g][:, 0:width, :].rearrange("p n t -> p (n t)"),
            )

        def mm(u, g, i):
            n0, width = subs[u]
            v, cols = w_cols(u, g)
            rows = slice(P * i, P * (i + 1))
            if g == 0:
                tag = "acc" if i < 4 else "bank"
                acc[u, i] = psum.tile([P, CW], F32, name=tag, tag=tag)
            if g == (3, 2, 0, 0)[u]:
                nc.tensor.matmul_mx(
                    out=acc[u, i][:, 0:width],
                    lhsT=hq[:, rows].bitcast(MX),
                    lhsT_scale=hqs[:, rows],
                    rhs=bq[n0 // CW][:, cols].bitcast(MX),
                    rhs_scale=bqs[n0 // CW][:, cols],
                    start=(u > 1),
                    stop=False,
                )
            nc.tensor.matmul_mx(
                out=acc[u, i][:, 0:width],
                lhsT=xq[:, g, rows].bitcast(MX),
                lhsT_scale=xqs[:, g, rows],
                rhs=wq[v][:, cols].bitcast(MX),
                rhs_scale=wqs[v][:, cols],
                start=(g == 0 and u < 2),
                stop=(g == G - 1),
            )

        def y_out(u, i):
            n0, width = subs[u]
            cols = slice(n0, n0 + width)
            res = resp.tile([P, CW], F32, name="res")
            nc.vector.tensor_tensor(out=res[:, 0:width], in0=acc[u, i][:, 0:width], in1=sb[:, cols], op=MULT)
            nc.sync.dma_start(out=out_view[:, i, cols], in_=res[:, 0:width])

        with tc.manual_schedule(
            engines={mybir.EngineType.PE, mybir.EngineType.DVE, mybir.EngineType.Activation, mybir.EngineType.SP}
        ):
            units = PAIRS * G
            for s in range(units + 3):
                if s < units:
                    x_widen(s)
                    x_turn(s)
                if s == 9:
                    nc.vector.reciprocal(out=rec[:], in_=normb[:])
                    nc.vector.tensor_tensor(out=s1[:], in0=magb[:], in1=rec[:], op=MULT)
                if 1 <= s <= units:
                    x_out(s - 1)
                if s < 8:
                    for t in range(2 * (s % 2), 2 * (s % 2) + 2):
                        a_inter(s // 2, t, "v" if t == 3 or (s == 6 and t == 1) else "s")
                if s >= 3:
                    x_quant(s - 3)
                if s >= 3 and s % 2 == 1 and s <= 9:
                    a_quant((s - 3) // 2)
                if s == 10:
                    nc.sync.dma_start(out=out[0].rearrange("(p j) -> p j", j=N // P), in_=s1[:])
                    nc.sync.dma_start(out=sb[:], in_=out[0].partition_broadcast(P))
                if s in (10, 12, 15):
                    h_mm({10: 0, 12: 1, 15: 2}[s])
                if s in (11, 13, 16):
                    h_out({11: 0, 13: 1, 16: 2}[s])
                if s in (13, 15, 18):
                    h_inter({13: 0, 15: 1, 18: 2}[s])
                if s in (14, 16):
                    h_quant({14: 0, 16: 1}[s])
                if s in (8, 9, 10, 11, 12, 14, 15, 16, 17, 18):
                    n = (8, 9, 10, 11, 12, 14, 15, 16, 17, 18).index(s)
                    w_widen(n // 2, (n % 2,))
                if s in (11, 12, 13, 14, 16, 17):
                    n = (11, 12, 13, 14, 16, 17).index(s)
                    w_inter(0, n // 2, "v", range(2 * (n % 2), 2 * (n % 2) + 2))
                if s == 13:
                    w_quant(0, 0)
                if s == 15:
                    w_quant(0, 1)
                if s == 18:
                    w_quant(0, 2)
                if s == 14:
                    for i in range(4):
                        mm(0, 0, i)
                if s == 16:
                    for i in range(4):
                        mm(0, 1, i)
                if s == 17:
                    b_inter(0, "v")
            h_mm(3)
            for i in range(4):
                mm(0, 2, i)
            h_quant(2)
            b_quant(0)
            w_inter(0, 3, "v", range(4))
            w_widen(5)
            h_out(3)
            for g in range(3):
                for i in range(4, TILES):
                    mm(0, g, i)
            todo = [(u, g) for u in range(1, len(subs)) for g in range(G)]

            def s_ahead(n):
                if n < len(todo):
                    u, g = todo[n]
                    v = w_cols(u, g)[0]
                    if u < 3 and v + 1 < C * G:
                        w_widen(v + 1)
                    w_inter(u, g, "s", range(own(u, g), subs[u][1] // 128))

            def own(u, g):
                n = subs[u][1] // 128
                return n - 1

            s_ahead(0)
            w_inter(1, 0, "v", range(own(1, 0)))
            h_inter(3)
            w_quant(0, 3)
            h_quant(3)
            for i in range(TILES):
                mm(0, 3, i)
            for n, (u, g) in enumerate(todo):
                if n > 0:
                    w_inter(u, g, "v", range(own(u, g)))
                s_ahead(n + 1)
                if (u, g) == (1, 0):
                    b_inter(1, "s")
                if (u, g) == (1, 2):
                    b_quant(1)
                    b_inter(2, "s")
                if (u, g) == (2, 0):
                    b_quant(2)
                if n == 0:
                    continue
                pu, pg = todo[n - 1]
                w_quant(pu, pg)
                if g == 1:
                    for i in range(TILES):
                        y_out(u - 1, i)
                        mm(pu, pg, i)
                else:
                    for i in range(TILES):
                        mm(pu, pg, i)
            w_quant(3, 3)
            for i in range(TILES):
                mm(3, 3, i)
                y_out(3, i)
